import numpy as np
import ml_dtypes


def mxq(x, axis, fmt="e4m3"):
    dtype, down = {"e4m3": (ml_dtypes.float8_e4m3fn, 7), "e5m2": (ml_dtypes.float8_e5m2, 14)}[fmt]
    v = np.moveaxis(np.asarray(x, np.float32).astype(ml_dtypes.bfloat16).astype(np.float64), axis, -1)
    blocks = v.reshape(v.shape[:-1] + (-1, 32))
    amax = np.abs(blocks).max(-1, keepdims=True)
    byte = np.maximum(np.where(amax > 0, np.frexp(amax)[1] - 1 + 127, 0) - down, 1)
    scale = np.exp2(byte - 127.0)
    codes = (blocks / scale).astype(np.float32).astype(dtype).astype(np.float64)
    return np.moveaxis((codes * scale).reshape(v.shape), -1, axis)


WIDE = False


def mx_kscale(k):
    if not WIDE:
        return np.ones(k)
    levels = np.array([10, -10, 5, -5, 0])
    if k % 512:
        return np.exp2(np.random.permutation(np.resize(levels, k // 32))).repeat(32)
    a = np.empty((k // 512, 16))
    for p in range(k // 512):
        a[p, :8] = np.random.permutation(np.resize(levels, 8))
        for g in range(8):
            far = levels[np.abs(levels - a[p, g]) >= 10]
            a[p, g + 8] = far[np.random.randint(len(far))]
    return np.exp2(a.ravel()).repeat(32)


def f64(x):
    return np.asarray(x).astype(np.float64)


def striped(idx):
    return np.tile(idx.reshape(-1, 16).T, (8, 1)).astype(np.uint16)


def unstriped(offs):
    return offs[:16].T.reshape(-1).astype(np.int64)


def pack_weight(w):
    k, n = w.shape
    w = f64(np.asarray(w, np.float32).astype(ml_dtypes.bfloat16)).reshape(k // 32, 32, n)
    amax = np.abs(w).max(1)
    byte = np.clip(np.where(amax > 0, np.frexp(amax)[1] - 1 + 127 - 7, 1), 1, 254)
    scaled = (w * np.exp2(127.0 - byte)[:, None, :]).reshape(k, n).astype(np.float32)
    words = np.ascontiguousarray(scaled.reshape(k // 512, 128, 4, n).transpose(0, 1, 3, 2)).astype(ml_dtypes.float8_e4m3fn).view(np.uint8)
    return words, np.ascontiguousarray(byte.astype(np.uint8).reshape(k // 512, 16, n))


def unpack_weight(words, scales):
    g, p, n, _ = words.shape
    vals = np.ascontiguousarray(words).view(ml_dtypes.float8_e4m3fn).astype(np.float64) * np.repeat(np.exp2(scales.astype(np.float64) - 127.0), 8, axis=1)[..., None]
    return vals.transpose(0, 1, 3, 2).reshape(g * 512, n)


K, T, S, N, U, D = 1024, 1024, 512, 128, 256, 4
P = 2 ** 7


def setup_inputs():
    n = np.random.standard_normal
    s = mx_kscale(K)[:, None]
    packed_xT = pack_weight(n((K, T)) * s)
    return {
        "x_words": packed_xT[0],
        "x_scales": packed_xT[1],
        "w1": (n((K, N)) / np.sqrt(K) / s).astype(np.float32),
        "wgt": (np.tile(np.random.uniform(0.1, 0.4, (D, 1, U)), (1, P, 1))).astype(np.float32),
        "old": (n((N, S))).astype(np.float32),
        "vel": (n((N, U))).astype(np.float32),
        "offs": striped(np.random.permutation(T)[:S]),
        "cor1": striped(np.random.randint(0, S, U)),
        "cor2": striped(np.random.randint(0, S, U)),
        "cor3": striped(np.random.randint(0, S, U)),
        "cor4": striped(np.random.randint(0, S, U)),
    }


def reference(x_words, x_scales, w1, wgt, old, vel, offs, cor1, cor2, cor3, cor4):
    xq = unpack_weight(x_words, x_scales)[:, unstriped(offs)]
    y = mxq(f64(w1), 0, "e4m3").T @ xq
    g0 = y[:, unstriped(cor1)]
    g1 = y[:, unstriped(cor2)]
    g2 = y[:, unstriped(cor3)]
    g3 = y[:, unstriped(cor4)]
    pic = g0 * f64(wgt)[0, :1] + g1 * f64(wgt)[1, :1] + g2 * f64(wgt)[2, :1] + g3 * f64(wgt)[3, :1]
    return 0.3 * pic + 0.7 * (f64(vel) + pic - (f64(old)[:, unstriped(cor1)] * f64(wgt)[0, :1] + f64(old)[:, unstriped(cor2)] * f64(wgt)[1, :1] + f64(old)[:, unstriped(cor3)] * f64(wgt)[2, :1] + f64(old)[:, unstriped(cor4)] * f64(wgt)[3, :1]))

@@ -1,0 +1,111 @@
+from contextlib import ExitStack
+
+import concourse.mybir as mybir
+
+K, T, S, N, U, D = 1024, 1024, 512, 128, 256, 4
+FLOPS = 2 * K * N * S
+F32 = mybir.dt.float32
+BF16 = mybir.dt.bfloat16
+U32 = mybir.dt.uint32
+I32 = mybir.dt.int32
+U16 = mybir.dt.uint16
+U8 = mybir.dt.uint8
+FP8X4 = mybir.dt.float8_e4m3fn_x4
+MULT = mybir.AluOpType.mult
+ADD = mybir.AluOpType.add
+COPY = mybir.ActivationFunctionType.Copy
+P = 128
+PACK = 4
+PASSES = K // (P * PACK)
+HALF = S // 2
+CHUNKS = U // P
+
+
+def tile_picked_yflip_flip_p_kernel(tc, x_words, x_scales, w1, wgt, old, vel, offs, cor1, cor2, cor3, cor4, out):
+    nc = tc.nc
+    with ExitStack() as ctx:
+        keep = ctx.enter_context(tc.tile_pool(name="keep", bufs=1))
+        psum = ctx.enter_context(tc.psum_pool(name="psum", bufs=1))
+
+        offs_sb = keep.tile([P, S // 16], U16, name="offs_sb")
+        nc.sync.dma_start(offs_sb[:], offs)
+
+        words = [keep.tile([P, T], U32, name=f"words{o}", align_bytes=64) for o in range(PASSES)]
+        nc.sync.dma_start(words[0][:].bitcast(I32), x_words[0].rearrange("p n t -> p (n t)").bitcast(I32))
+
+        planes = keep.tile([P, T], U8, name="planes", align_bytes=64)
+        nc.gpsimd.memset(planes[:].bitcast(I32), 0)
+        for q in range(4):
+            nc.sync.dma_start(planes[32 * q : 32 * q + 4 * PASSES, :].bitcast(I32), x_scales[:, 4 * q : 4 * q + 4, :].bitcast(I32))
+
+        w_raw = [keep.tile([P, PACK, N], F32, name=f"w_raw{o}", tag=f"staged{o}", align_bytes=64) for o in range(PASSES)]
+        for o in range(PASSES):
+            nc.sync.dma_start(w_raw[o][:], w1[o * P * PACK : (o + 1) * P * PACK, :].rearrange("(p j) m -> p j m", j=PACK))
+        nc.sync.dma_start(words[1][:].bitcast(I32), x_words[1].rearrange("p n t -> p (n t)").bitcast(I32))
+
+        old_sb = keep.tile([P, S], F32, name="old_sb")
+        nc.sync.dma_start(old_sb[:], old)
+        cors = []
+        for d, cor in enumerate((cor1, cor2, cor3, cor4)):
+            cor_sb = keep.tile([P, U // 16], U16, name=f"cor_sb{d}")
+            nc.sync.dma_start(cor_sb[:], cor)
+            cors.append(cor_sb)
+        wgt_sb = keep.tile([P, D, U], F32, name="wgt_sb")
+        nc.sync.dma_start(wgt_sb[:], wgt.rearrange("d p r -> p d r"))
+        vel_sb = keep.tile([P, U], F32, name="vel_sb")
+        nc.sync.dma_start(vel_sb[:], vel)
+
+        picked_planes = keep.tile([P, S], U8, name="picked_planes", align_bytes=64)
+        nc.vector.tensor_copy(picked_planes[:], planes[:].indirect(offs_sb[:]))
+
+        picked_first = keep.tile([P, S], U32, name="picked_first", align_bytes=64)
+        nc.vector.tensor_copy(picked_first[:], words[0][:].indirect(offs_sb[:]))
+        picked = [[picked_first[:, h * HALF : (h + 1) * HALF] for h in range(2)], []]
+        grouped = keep.tile([P, PASSES, N, PACK], BF16, name="grouped", align_bytes=64)
+        for o in range(PASSES):
+            nc.scalar.copy(grouped[:, o], w_raw[o][:].rearrange("p j m -> p m j"))
+        w_codes = keep.tile([P, PASSES, N], U32, name="w_codes", align_bytes=64)
+        w_plane = keep.tile([P, PASSES, N], U8, name="w_plane", align_bytes=64)
+        nc.vector.quantize_mx(
+            out=w_codes[:].rearrange("p o m -> p (o m)").bitcast(FP8X4),
+            scales=w_plane[:].rearrange("p o m -> p (o m)"),
+            in_=grouped[:].rearrange("p o m j -> p (o m j)"),
+        )
+        picked_second = keep.tile([P, S], U32, name="picked_second", tag="staged1", align_bytes=64)
+        for h in range(2):
+            picked[1].append(picked_second[:, h * HALF : (h + 1) * HALF])
+            nc.vector.tensor_copy(picked[1][h], words[1][:].indirect(offs_sb[:, h * HALF // 16 : (h + 1) * HALF // 16]))
+
+        banks = [psum.tile([P, HALF], F32, name=f"bank{h}") for h in range(2)]
+        for o in range(PASSES):
+            for h in range(2):
+                nc.tensor.matmul_mx(
+                    banks[h][:],
+                    lhsT=w_codes[:, o, :].bitcast(FP8X4),
+                    lhsT_scale=w_plane[:, o, :],
+                    rhs=picked[o][h].bitcast(FP8X4),
+                    rhs_scale=picked_planes[4 * o :, h * HALF : (h + 1) * HALF],
+                    start=(o == 0),
+                    stop=(o == PASSES - 1),
+                )
+
+        z = keep.tile([P, S], F32, name="z")
+        for h in range(2):
+            cols = slice(h * HALF, (h + 1) * HALF)
+            nc.vector.scalar_tensor_tensor(z[:, cols], old_sb[:, cols], -0.7, banks[h][:], MULT, ADD)
+
+        terms = [keep.tile([P, U], F32, name=f"term{d}") for d in range(D)]
+        for d in range(D):
+            nc.vector.tensor_tensor(terms[d][:], z[:].indirect(cors[d][:]), wgt_sb[:, d, :], MULT)
+        with_vel = keep.tile([P, U], F32, name="with_vel")
+        nc.vector.scalar_tensor_tensor(with_vel[:], vel_sb[:], 0.7, terms[0][:], MULT, ADD)
+        middle = keep.tile([P, U], F32, name="middle")
+        nc.vector.tensor_tensor(middle[:], terms[1][:], terms[2][:], ADD)
+        outer = keep.tile([P, U], F32, name="outer")
+        result = keep.tile([P, U], F32, name="result")
+        halves = [slice(c * P, (c + 1) * P) for c in range(CHUNKS)]
+        for cols in halves:
+            nc.vector.tensor_tensor(outer[:, cols], with_vel[:, cols], terms[3][:, cols], ADD)
+        for cols in halves:
+            nc.vector.tensor_tensor(result[:, cols], outer[:, cols], middle[:, cols], ADD)
+        nc.sync.dma_start(out, result[:])

@@ -19,6 +19,7 @@ PACK = 4
 PASSES = K // (P * PACK)
 HALF = S // 2
 CHUNKS = U // P
+PIECES = ((0, 256), (256, 384), (384, 512))
 
 
 def tile_picked_yflip_flip_p_kernel(tc, x_words, x_scales, w1, wgt, old, vel, offs, cor1, cor2, cor3, cor4, out):
@@ -47,11 +48,11 @@ def tile_picked_yflip_flip_p_kernel(tc, x_words, x_scales, w1, wgt, old, vel, of
         nc.sync.dma_start(old_sb[:], old)
         cors = []
         for d, cor in enumerate((cor1, cor2, cor3, cor4)):
-            cor_sb = keep.tile([P, U // 16], U16, name=f"cor_sb{d}")
-            nc.sync.dma_start(cor_sb[:], cor)
-            cors.append(cor_sb)
-        wgt_sb = keep.tile([P, D, U], F32, name="wgt_sb")
-        nc.sync.dma_start(wgt_sb[:], wgt.rearrange("d p r -> p d r"))
+            cors.append(keep.tile([P, U // 16], U16, name=f"cor_sb{d}"))
+            nc.sync.dma_start(cors[d][:], cor)
+        wgt_sb = [keep.tile([P, 2, U], F32, name=f"wgt_sb{i}") for i in range(D // 2)]
+        for i in range(D // 2):
+            nc.sync.dma_start(wgt_sb[i][:], wgt[2 * i : 2 * i + 2].rearrange("d p r -> p d r"))
         vel_sb = keep.tile([P, U], F32, name="vel_sb")
         nc.sync.dma_start(vel_sb[:], vel)
 
@@ -60,10 +61,9 @@ def tile_picked_yflip_flip_p_kernel(tc, x_words, x_scales, w1, wgt, old, vel, of
 
         picked_first = keep.tile([P, S], U32, name="picked_first", align_bytes=64)
         nc.vector.tensor_copy(picked_first[:], words[0][:].indirect(offs_sb[:]))
-        picked = [[picked_first[:, h * HALF : (h + 1) * HALF] for h in range(2)], []]
         grouped = keep.tile([P, PASSES, N, PACK], BF16, name="grouped", align_bytes=64)
         for o in range(PASSES):
-            nc.scalar.copy(grouped[:, o], w_raw[o][:].rearrange("p j m -> p m j"))
+            nc.scalar.copy(grouped[:, o].rearrange("p (c i) j -> p c j i", i=4), w_raw[o][:].rearrange("p j (c i) -> p c j i", i=4))
         w_codes = keep.tile([P, PASSES, N], U32, name="w_codes", align_bytes=64)
         w_plane = keep.tile([P, PASSES, N], U8, name="w_plane", align_bytes=64)
         nc.vector.quantize_mx(
@@ -72,40 +72,39 @@ def tile_picked_yflip_flip_p_kernel(tc, x_words, x_scales, w1, wgt, old, vel, of
             in_=grouped[:].rearrange("p o m j -> p (o m j)"),
         )
         picked_second = keep.tile([P, S], U32, name="picked_second", tag="staged1", align_bytes=64)
-        for h in range(2):
-            picked[1].append(picked_second[:, h * HALF : (h + 1) * HALF])
-            nc.vector.tensor_copy(picked[1][h], words[1][:].indirect(offs_sb[:, h * HALF // 16 : (h + 1) * HALF // 16]))
+        for lo, hi in PIECES:
+            nc.vector.tensor_copy(picked_second[:, lo:hi], words[1][:].indirect(offs_sb[:, lo // 16 : hi // 16]))
+        picked = [picked_first, picked_second]
 
-        banks = [psum.tile([P, HALF], F32, name=f"bank{h}") for h in range(2)]
+        banks = [psum.tile([P, hi - lo], F32, name=f"y_bank{i}", tag=f"y_bank{i}") for i, (lo, hi) in enumerate(PIECES)]
         for o in range(PASSES):
-            for h in range(2):
+            for bank, (lo, hi) in zip(banks, PIECES):
                 nc.tensor.matmul_mx(
-                    banks[h][:],
+                    bank[:],
                     lhsT=w_codes[:, o, :].bitcast(FP8X4),
                     lhsT_scale=w_plane[:, o, :],
-                    rhs=picked[o][h].bitcast(FP8X4),
-                    rhs_scale=picked_planes[4 * o :, h * HALF : (h + 1) * HALF],
+                    rhs=picked[o][:, lo:hi].bitcast(FP8X4),
+                    rhs_scale=picked_planes[4 * o :, lo:hi],
                     start=(o == 0),
                     stop=(o == PASSES - 1),
                 )
 
         z = keep.tile([P, S], F32, name="z")
-        for h in range(2):
-            cols = slice(h * HALF, (h + 1) * HALF)
-            nc.vector.scalar_tensor_tensor(z[:, cols], old_sb[:, cols], -0.7, banks[h][:], MULT, ADD)
+        for bank, (lo, hi) in zip(banks, PIECES):
+            nc.vector.scalar_tensor_tensor(z[:, lo:hi], old_sb[:, lo:hi], -0.7, bank[:], MULT, ADD)
 
+        halves = [slice(c * P, (c + 1) * P) for c in range(CHUNKS)]
         terms = [keep.tile([P, U], F32, name=f"term{d}") for d in range(D)]
         for d in range(D):
-            nc.vector.tensor_tensor(terms[d][:], z[:].indirect(cors[d][:]), wgt_sb[:, d, :], MULT)
+            nc.vector.tensor_tensor(terms[d][:], z[:].indirect(cors[d][:]), wgt_sb[d // 2][:, d % 2, :], MULT)
         with_vel = keep.tile([P, U], F32, name="with_vel")
         nc.vector.scalar_tensor_tensor(with_vel[:], vel_sb[:], 0.7, terms[0][:], MULT, ADD)
         middle = keep.tile([P, U], F32, name="middle")
         nc.vector.tensor_tensor(middle[:], terms[1][:], terms[2][:], ADD)
         outer = keep.tile([P, U], F32, name="outer")
-        result = keep.tile([P, U], F32, name="result")
-        halves = [slice(c * P, (c + 1) * P) for c in range(CHUNKS)]
         for cols in halves:
             nc.vector.tensor_tensor(outer[:, cols], with_vel[:, cols], terms[3][:, cols], ADD)
-        for cols in halves:
-            nc.vector.tensor_tensor(result[:, cols], outer[:, cols], middle[:, cols], ADD)
-        nc.sync.dma_start(out, result[:])
+        for c, cols in enumerate(halves):
+            result = keep.tile([P, P], F32, name=f"result{c}")
+            nc.vector.tensor_tensor(result[:], outer[:, cols], middle[:, cols], ADD)
+            nc.sync.dma_start(out[:, cols], result[:])

@@ -1,6 +1,7 @@
 from contextlib import ExitStack
 
 import concourse.mybir as mybir
+from concourse.masks import make_identity
 
 K, T, S, N, U, D = 1024, 1024, 512, 128, 256, 4
 FLOPS = 2 * K * N * S
@@ -50,18 +51,21 @@ def tile_picked_yflip_flip_p_kernel(tc, x_words, x_scales, w1, wgt, old, vel, of
         for d, cor in enumerate((cor1, cor2, cor3, cor4)):
             cors.append(keep.tile([P, U // 16], U16, name=f"cor_sb{d}"))
             nc.sync.dma_start(cors[d][:], cor)
+        vel_sb = keep.tile([P, U], F32, name="vel_sb")
+        nc.sync.dma_start(vel_sb[:], vel)
         wgt_sb = [keep.tile([P, 2, U], F32, name=f"wgt_sb{i}") for i in range(D // 2)]
         for i in range(D // 2):
             nc.sync.dma_start(wgt_sb[i][:], wgt[2 * i : 2 * i + 2].rearrange("d p r -> p d r"))
-        vel_sb = keep.tile([P, U], F32, name="vel_sb")
-        nc.sync.dma_start(vel_sb[:], vel)
+
+        ident = keep.tile([P, P], F32, name="ident")
+        make_identity(nc, ident[:])
 
         picked_planes = keep.tile([P, S], U8, name="picked_planes", align_bytes=64)
         nc.vector.tensor_copy(picked_planes[:], planes[:].indirect(offs_sb[:]))
 
         picked_first = keep.tile([P, S], U32, name="picked_first", align_bytes=64)
         nc.vector.tensor_copy(picked_first[:], words[0][:].indirect(offs_sb[:]))
-        grouped = keep.tile([P, PASSES, N, PACK], BF16, name="grouped", align_bytes=64)
+        grouped = keep.tile([P, PASSES, N, PACK], BF16, name="grouped", tag="grouped", align_bytes=64)
         for o in range(PASSES):
             nc.scalar.copy(grouped[:, o].rearrange("p (c i) j -> p c j i", i=4), w_raw[o][:].rearrange("p j (c i) -> p c j i", i=4))
         w_codes = keep.tile([P, PASSES, N], U32, name="w_codes", align_bytes=64)
@@ -94,17 +98,36 @@ def tile_picked_yflip_flip_p_kernel(tc, x_words, x_scales, w1, wgt, old, vel, of
             nc.vector.scalar_tensor_tensor(z[:, lo:hi], old_sb[:, lo:hi], -0.7, bank[:], MULT, ADD)
 
         halves = [slice(c * P, (c + 1) * P) for c in range(CHUNKS)]
+        turned_sums = [psum.tile([P, P], F32, name=f"turned_sum{c}") for c in range(CHUNKS)]
+
+        def add_turned(c, values, start, stop):
+            nc.tensor.matmul(turned_sums[c][:], values, ident[:], start=start, stop=stop, is_transpose=True)
+
+        vel_scaled = keep.tile([P, U], F32, name="vel_scaled", tag="grouped", align_bytes=64)
+        nc.scalar.activation(vel_scaled[:], vel_sb[:], COPY, scale=0.7)
+        for c, cols in enumerate(halves):
+            add_turned(c, vel_scaled[:, cols], True, False)
+
         terms = [keep.tile([P, U], F32, name=f"term{d}") for d in range(D)]
-        for d in range(D):
-            nc.vector.tensor_tensor(terms[d][:], z[:].indirect(cors[d][:]), wgt_sb[d // 2][:, d % 2, :], MULT)
-        with_vel = keep.tile([P, U], F32, name="with_vel")
-        nc.vector.scalar_tensor_tensor(with_vel[:], vel_sb[:], 0.7, terms[0][:], MULT, ADD)
-        middle = keep.tile([P, U], F32, name="middle")
-        nc.vector.tensor_tensor(middle[:], terms[1][:], terms[2][:], ADD)
-        outer = keep.tile([P, U], F32, name="outer")
+        nc.vector.tensor_tensor(terms[0][:], z[:].indirect(cors[0][:]), wgt_sb[0][:, 0, :], MULT)
+        for c, cols in enumerate(halves):
+            add_turned(c, terms[0][:, cols], False, False)
+        sums = []
+        for c, cols in enumerate(halves):
+            nc.vector.tensor_tensor(terms[1][:, cols], z[:].indirect(cors[1][:, c * P // 16 : (c + 1) * P // 16]), wgt_sb[0][:, 1, cols], MULT)
+            add_turned(c, terms[1][:, cols], False, True)
+        for c in range(CHUNKS):
+            staged_sum = keep.tile([P, P], F32, name=f"staged_sum{c}")
+            nc.scalar.copy(staged_sum[:], turned_sums[c][:])
+            sums.append(psum.tile([P, P], F32, name=f"sum{c}"))
+            nc.tensor.transpose(sums[c][:], staged_sum[:], ident[:])
+
+        for d in range(2, D):
+            nc.vector.tensor_tensor(terms[d][:], z[:].indirect(cors[d][:]), wgt_sb[1][:, d - 2, :], MULT)
+        later = keep.tile([P, U], F32, name="later")
         for cols in halves:
-            nc.vector.tensor_tensor(outer[:, cols], with_vel[:, cols], terms[3][:, cols], ADD)
+            nc.vector.tensor_tensor(later[:, cols], terms[2][:, cols], terms[3][:, cols], ADD)
         for c, cols in enumerate(halves):
             result = keep.tile([P, P], F32, name=f"result{c}")
-            nc.vector.tensor_tensor(result[:], outer[:, cols], middle[:, cols], ADD)
+            nc.vector.tensor_tensor(result[:], sums[c][:], later[:, cols], ADD)
             nc.sync.dma_start(out[:, cols], result[:])

@@ -32,18 +32,23 @@ def tile_picked_yflip_flip_p_kernel(tc, x_words, x_scales, w1, wgt, old, vel, of
         offs_sb = keep.tile([P, S // 16], U16, name="offs_sb")
         nc.sync.dma_start(offs_sb[:], offs)
 
+        w_raw = [keep.tile([P, PACK, N], F32, name=f"w_raw{o}", tag=f"staged{o}", align_bytes=64) for o in range(PASSES)]
         words = [keep.tile([P, T], U32, name=f"words{o}", align_bytes=64) for o in range(PASSES)]
-        nc.sync.dma_start(words[0][:].bitcast(I32), x_words[0].rearrange("p n t -> p (n t)").bitcast(I32))
 
+        def load_w(o):
+            nc.sync.dma_start(w_raw[o][:], w1[o * P * PACK : (o + 1) * P * PACK, :].rearrange("(p j) m -> p j m", j=PACK))
+
+        def load_words(o):
+            nc.sync.dma_start(words[o][:].bitcast(I32), x_words[o].rearrange("p n t -> p (n t)").bitcast(I32))
+
+        load_w(0)
         planes = keep.tile([P, T], U8, name="planes", align_bytes=64)
         nc.gpsimd.memset(planes[:].bitcast(I32), 0)
         for q in range(4):
             nc.sync.dma_start(planes[32 * q : 32 * q + 4 * PASSES, :].bitcast(I32), x_scales[:, 4 * q : 4 * q + 4, :].bitcast(I32))
-
-        w_raw = [keep.tile([P, PACK, N], F32, name=f"w_raw{o}", tag=f"staged{o}", align_bytes=64) for o in range(PASSES)]
-        for o in range(PASSES):
-            nc.sync.dma_start(w_raw[o][:], w1[o * P * PACK : (o + 1) * P * PACK, :].rearrange("(p j) m -> p j m", j=PACK))
-        nc.sync.dma_start(words[1][:].bitcast(I32), x_words[1].rearrange("p n t -> p (n t)").bitcast(I32))
+        load_words(0)
+        load_w(1)
+        load_words(1)
 
         old_sb = keep.tile([P, S], F32, name="old_sb")
         nc.sync.dma_start(old_sb[:], old)
@@ -63,11 +68,11 @@ def tile_picked_yflip_flip_p_kernel(tc, x_words, x_scales, w1, wgt, old, vel, of
         picked_planes = keep.tile([P, S], U8, name="picked_planes", align_bytes=64)
         nc.vector.tensor_copy(picked_planes[:], planes[:].indirect(offs_sb[:]))
 
-        picked_first = keep.tile([P, S], U32, name="picked_first", align_bytes=64)
-        nc.vector.tensor_copy(picked_first[:], words[0][:].indirect(offs_sb[:]))
         grouped = keep.tile([P, PASSES, N, PACK], BF16, name="grouped", tag="grouped", align_bytes=64)
         for o in range(PASSES):
             nc.scalar.copy(grouped[:, o].rearrange("p (c i) j -> p c j i", i=4), w_raw[o][:].rearrange("p j (c i) -> p c j i", i=4))
+        picked_first = keep.tile([P, S], U32, name="picked_first", tag="staged0", align_bytes=64)
+        nc.vector.tensor_copy(picked_first[:], words[0][:].indirect(offs_sb[:]))
         w_codes = keep.tile([P, PASSES, N], U32, name="w_codes", align_bytes=64)
         w_plane = keep.tile([P, PASSES, N], U8, name="w_plane", align_bytes=64)
         nc.vector.quantize_mx(
@@ -122,8 +127,9 @@ def tile_picked_yflip_flip_p_kernel(tc, x_words, x_scales, w1, wgt, old, vel, of
             sums.append(psum.tile([P, P], F32, name=f"sum{c}"))
             nc.tensor.transpose(sums[c][:], staged_sum[:], ident[:])
 
-        for d in range(2, D):
-            nc.vector.tensor_tensor(terms[d][:], z[:].indirect(cors[d][:]), wgt_sb[1][:, d - 2, :], MULT)
+        nc.vector.tensor_tensor(terms[2][:], z[:].indirect(cors[2][:]), wgt_sb[1][:, 0, :], MULT)
+        for c, cols in enumerate(halves):
+            nc.vector.tensor_tensor(terms[3][:, cols], z[:].indirect(cors[3][:, c * P // 16 : (c + 1) * P // 16]), wgt_sb[1][:, 1, cols], MULT)
         later = keep.tile([P, U], F32, name="later")
         for cols in halves:
             nc.vector.tensor_tensor(later[:, cols], terms[2][:, cols], terms[3][:, cols], ADD)

from contextlib import ExitStack

import concourse.mybir as mybir
from concourse.masks import make_identity

K, T, S, N, U, D = 1024, 1024, 512, 128, 256, 4
FLOPS = 2 * K * N * S
F32 = mybir.dt.float32
BF16 = mybir.dt.bfloat16
U32 = mybir.dt.uint32
I32 = mybir.dt.int32
U16 = mybir.dt.uint16
U8 = mybir.dt.uint8
FP8X4 = mybir.dt.float8_e4m3fn_x4
MULT = mybir.AluOpType.mult
ADD = mybir.AluOpType.add
COPY = mybir.ActivationFunctionType.Copy
P = 128
PACK = 4
PASSES = K // (P * PACK)
HALF = S // 2
CHUNKS = U // P
PIECES = ((0, 256), (256, 384), (384, 512))


def tile_picked_yflip_flip_p_kernel(tc, x_words, x_scales, w1, wgt, old, vel, offs, cor1, cor2, cor3, cor4, out):
    nc = tc.nc
    with ExitStack() as ctx:
        keep = ctx.enter_context(tc.tile_pool(name="keep", bufs=1))
        psum = ctx.enter_context(tc.psum_pool(name="psum", bufs=1))

        offs_sb = keep.tile([P, S // 16], U16, name="offs_sb")
        nc.sync.dma_start(offs_sb[:], offs)

        w_raw = [keep.tile([P, PACK, N], F32, name=f"w_raw{o}", tag=f"staged{o}", align_bytes=64) for o in range(PASSES)]
        words = [keep.tile([P, T], U32, name=f"words{o}", align_bytes=64) for o in range(PASSES)]

        def load_w(o):
            nc.sync.dma_start(w_raw[o][:], w1[o * P * PACK : (o + 1) * P * PACK, :].rearrange("(p j) m -> p j m", j=PACK))

        def load_words(o):
            nc.sync.dma_start(words[o][:].bitcast(I32), x_words[o].rearrange("p n t -> p (n t)").bitcast(I32))

        load_w(0)
        planes = keep.tile([P, T], U8, name="planes", align_bytes=64)
        nc.gpsimd.memset(planes[:].bitcast(I32), 0)
        for q in range(4):
            nc.sync.dma_start(planes[32 * q : 32 * q + 4 * PASSES, :].bitcast(I32), x_scales[:, 4 * q : 4 * q + 4, :].bitcast(I32))
        load_words(0)
        load_w(1)
        load_words(1)

        old_sb = keep.tile([P, S], F32, name="old_sb")
        nc.sync.dma_start(old_sb[:], old)
        cors = []
        for d, cor in enumerate((cor1, cor2, cor3, cor4)):
            cors.append(keep.tile([P, U // 16], U16, name=f"cor_sb{d}"))
            nc.sync.dma_start(cors[d][:], cor)
        vel_sb = keep.tile([P, U], F32, name="vel_sb")
        nc.sync.dma_start(vel_sb[:], vel)
        wgt_sb = [keep.tile([P, 2, U], F32, name=f"wgt_sb{i}") for i in range(D // 2)]
        for i in range(D // 2):
            nc.sync.dma_start(wgt_sb[i][:], wgt[2 * i : 2 * i + 2].rearrange("d p r -> p d r"))

        ident = keep.tile([P, P], F32, name="ident")
        make_identity(nc, ident[:])

        picked_planes = keep.tile([P, S], U8, name="picked_planes", align_bytes=64)
        nc.vector.tensor_copy(picked_planes[:], planes[:].indirect(offs_sb[:]))

        grouped = keep.tile([P, PASSES, N, PACK], BF16, name="grouped", tag="grouped", align_bytes=64)
        for o in range(PASSES):
            nc.scalar.copy(grouped[:, o].rearrange("p (c i) j -> p c j i", i=4), w_raw[o][:].rearrange("p j (c i) -> p c j i", i=4))
        picked_first = keep.tile([P, S], U32, name="picked_first", tag="staged0", align_bytes=64)
        nc.vector.tensor_copy(picked_first[:], words[0][:].indirect(offs_sb[:]))
        w_codes = keep.tile([P, PASSES, N], U32, name="w_codes", align_bytes=64)
        w_plane = keep.tile([P, PASSES, N], U8, name="w_plane", align_bytes=64)
        nc.vector.quantize_mx(
            out=w_codes[:].rearrange("p o m -> p (o m)").bitcast(FP8X4),
            scales=w_plane[:].rearrange("p o m -> p (o m)"),
            in_=grouped[:].rearrange("p o m j -> p (o m j)"),
        )
        picked_second = keep.tile([P, S], U32, name="picked_second", tag="staged1", align_bytes=64)
        for lo, hi in PIECES:
            nc.vector.tensor_copy(picked_second[:, lo:hi], words[1][:].indirect(offs_sb[:, lo // 16 : hi // 16]))
        picked = [picked_first, picked_second]

        banks = [psum.tile([P, hi - lo], F32, name=f"y_bank{i}", tag=f"y_bank{i}") for i, (lo, hi) in enumerate(PIECES)]
        for o in range(PASSES):
            for bank, (lo, hi) in zip(banks, PIECES):
                nc.tensor.matmul_mx(
                    bank[:],
                    lhsT=w_codes[:, o, :].bitcast(FP8X4),
                    lhsT_scale=w_plane[:, o, :],
                    rhs=picked[o][:, lo:hi].bitcast(FP8X4),
                    rhs_scale=picked_planes[4 * o :, lo:hi],
                    start=(o == 0),
                    stop=(o == PASSES - 1),
                )

        z = keep.tile([P, S], F32, name="z")
        for bank, (lo, hi) in zip(banks, PIECES):
            nc.vector.scalar_tensor_tensor(z[:, lo:hi], old_sb[:, lo:hi], -0.7, bank[:], MULT, ADD)

        halves = [slice(c * P, (c + 1) * P) for c in range(CHUNKS)]
        turned_sums = [psum.tile([P, P], F32, name=f"turned_sum{c}") for c in range(CHUNKS)]

        def add_turned(c, values, start, stop):
            nc.tensor.matmul(turned_sums[c][:], values, ident[:], start=start, stop=stop, is_transpose=True)

        vel_scaled = keep.tile([P, U], F32, name="vel_scaled", tag="grouped", align_bytes=64)
        nc.scalar.activation(vel_scaled[:], vel_sb[:], COPY, scale=0.7)
        for c, cols in enumerate(halves):
            add_turned(c, vel_scaled[:, cols], True, False)

        terms = [keep.tile([P, U], F32, name=f"term{d}") for d in range(D)]
        nc.vector.tensor_tensor(terms[0][:], z[:].indirect(cors[0][:]), wgt_sb[0][:, 0, :], MULT)
        for c, cols in enumerate(halves):
            add_turned(c, terms[0][:, cols], False, False)
        sums = []
        for c, cols in enumerate(halves):
            nc.vector.tensor_tensor(terms[1][:, cols], z[:].indirect(cors[1][:, c * P // 16 : (c + 1) * P // 16]), wgt_sb[0][:, 1, cols], MULT)
            add_turned(c, terms[1][:, cols], False, True)
        for c in range(CHUNKS):
            staged_sum = keep.tile([P, P], F32, name=f"staged_sum{c}")
            nc.scalar.copy(staged_sum[:], turned_sums[c][:])
            sums.append(psum.tile([P, P], F32, name=f"sum{c}"))
            nc.tensor.transpose(sums[c][:], staged_sum[:], ident[:])

        nc.vector.tensor_tensor(terms[2][:], z[:].indirect(cors[2][:]), wgt_sb[1][:, 0, :], MULT)
        for c, cols in enumerate(halves):
            nc.vector.tensor_tensor(terms[3][:, cols], z[:].indirect(cors[3][:, c * P // 16 : (c + 1) * P // 16]), wgt_sb[1][:, 1, cols], MULT)
        later = keep.tile([P, U], F32, name="later")
        for cols in halves:
            nc.vector.tensor_tensor(later[:, cols], terms[2][:, cols], terms[3][:, cols], ADD)
        for c, cols in enumerate(halves):
            result = keep.tile([P, P], F32, name=f"result{c}")
            nc.vector.tensor_tensor(result[:], sums[c][:], later[:, cols], ADD)
            nc.sync.dma_start(out[:, cols], result[:])
